import numpy as np
import ml_dtypes

BF16 = ml_dtypes.bfloat16


def bf(x):
    return np.asarray(x, np.float32).astype(BF16)


def f32(x):
    return np.asarray(x, np.float32)


def f64(x):
    return np.asarray(x).astype(np.float64)


def striped(idx):
    return np.tile(idx.reshape(-1, 16).T, (8, 1))


S, K, M, N, E, Q, H = 256, 256, 256, 256, 4, 64, 128


def sigmoid(v):
    return 1.0 / (1.0 + np.exp(-v))


def setup_inputs():
    return {"table": bf(np.random.standard_normal((K, S))), "w": bf(np.random.standard_normal((E, K, M)) / np.sqrt(K)), "offs": striped(np.sort(np.random.permutation(S).reshape(E, Q), axis=1).reshape(-1))}


def reference(table, w, offs):
    idx = offs[:16].T.reshape(-1)
    x = f64(table)[:, idx]
    y = np.concatenate([f64(w)[e].T @ x[:, e * Q : (e + 1) * Q] for e in range(E)], axis=1)
    return y[:H] * sigmoid(y[H:])

@@ -1,0 +1,67 @@
+import concourse.mybir as mybir
+
+BF16, F32, U16 = mybir.dt.bfloat16, mybir.dt.float32, mybir.dt.uint16
+SIGMOID = mybir.ActivationFunctionType.Sigmoid
+MULT = mybir.AluOpType.mult
+
+P = 128
+S = 256
+K = 256
+K_BLOCKS = K // P
+H = 128
+E = 4
+Q = 64
+N = E * Q
+Q_COLS = Q // 16
+
+WARM_MATMULS = 7
+WARM_COLUMNS = 256
+
+FLOPS = 2 * K * 2 * H * N
+
+
+def tile_gather_matmul_kernel(tc, table, w, offs, out):
+    nc = tc.nc
+    with (
+        tc.tile_pool(name="held", bufs=1) as held,
+        tc.psum_pool(name="psum", bufs=2) as psum,
+        tc.psum_pool(name="warm_psum", bufs=1) as warm_psum,
+    ):
+        offsets = held.tile([P, N // 16], U16, name="offsets")
+        nc.sync.dma_start(offsets[:], offs)
+
+        table_blocks = [held.tile([P, S], BF16, name=f"table{kb}") for kb in range(K_BLOCKS)]
+        weights = [held.tile([P, K_BLOCKS, 2 * H], BF16, name=f"w{e}") for e in range(E)]
+
+        for kb in range(K_BLOCKS):
+            nc.scalar.dma_start(table_blocks[kb][:], table[kb * P : (kb + 1) * P, :])
+            nc.sync.dma_start(weights[0][:, kb, :], w[0, kb * P : (kb + 1) * P, :])
+        for e in range(1, E):
+            nc.sync.dma_start(weights[e][:], w[e].rearrange("(kb p) m -> p kb m", p=P))
+
+        zeros = held.tile([P, WARM_COLUMNS], BF16, name="zeros")
+        nc.vector.memset(zeros[:], 0.0)
+        warm = warm_psum.tile([P, WARM_COLUMNS], F32, name="warm")
+        for i in range(WARM_MATMULS):
+            nc.tensor.matmul(warm[:], zeros[:, 0:P], zeros[:], start=True, stop=True)
+
+        for e in range(E):
+            picked = offsets[:, e * Q_COLS : (e + 1) * Q_COLS]
+
+            gate = psum.tile([P, Q], F32, name="gate")
+            value = psum.tile([P, Q], F32, name="value")
+            for bank, first_column in ((gate, H), (value, 0)):
+                for kb in range(K_BLOCKS):
+                    nc.tensor.matmul(
+                        bank[:],
+                        weights[e][:, kb, first_column : first_column + H],
+                        table_blocks[kb][:].indirect(picked),
+                        start=(kb == 0),
+                        stop=(kb == K_BLOCKS - 1),
+                    )
+
+            opened = held.tile([P, Q], F32, name=f"opened{e}")
+            nc.scalar.activation(opened[:], gate[:], SIGMOID)
+            gated = held.tile([P, Q], F32, name=f"gated{e}")
+            nc.vector.tensor_tensor(gated[:], value[:], opened[:], MULT)
+            nc.sync.dma_start(out[:, e * Q : (e + 1) * Q], gated[:])

@@ -24,8 +24,7 @@ def tile_gather_matmul_kernel(tc, table, w, offs, out):
     nc = tc.nc
     with (
         tc.tile_pool(name="held", bufs=1) as held,
-        tc.psum_pool(name="psum", bufs=2) as psum,
-        tc.psum_pool(name="warm_psum", bufs=1) as warm_psum,
+        tc.psum_pool(name="psum", bufs=E) as psum,
     ):
         offsets = held.tile([P, N // 16], U16, name="offsets")
         nc.sync.dma_start(offsets[:], offs)
@@ -41,15 +40,15 @@ def tile_gather_matmul_kernel(tc, table, w, offs, out):
 
         zeros = held.tile([P, WARM_COLUMNS], BF16, name="zeros")
         nc.vector.memset(zeros[:], 0.0)
-        warm = warm_psum.tile([P, WARM_COLUMNS], F32, name="warm")
+        warm = psum.tile([P, WARM_COLUMNS], F32, name="warm", tag="value")
         for i in range(WARM_MATMULS):
             nc.tensor.matmul(warm[:], zeros[:, 0:P], zeros[:], start=True, stop=True)
 
         for e in range(E):
             picked = offsets[:, e * Q_COLS : (e + 1) * Q_COLS]
 
-            gate = psum.tile([P, Q], F32, name="gate")
-            value = psum.tile([P, Q], F32, name="value")
+            gate = psum.tile([P, Q], F32, name="gate", tag="gate")
+            value = psum.tile([P, Q], F32, name="value", tag="value")
             for bank, first_column in ((gate, H), (value, 0)):
                 for kb in range(K_BLOCKS):
                     nc.tensor.matmul(

@@ -32,11 +32,13 @@ def tile_gather_matmul_kernel(tc, table, w, offs, out):
         table_blocks = [held.tile([P, S], BF16, name=f"table{kb}") for kb in range(K_BLOCKS)]
         weights = [held.tile([P, K_BLOCKS, 2 * H], BF16, name=f"w{e}") for e in range(E)]
 
+        table_by_block = table.rearrange("(p kb) s -> kb p s", kb=K_BLOCKS)
+        first_by_block = w[0].rearrange("(p kb) m -> kb p m", kb=K_BLOCKS)
         for kb in range(K_BLOCKS):
-            nc.scalar.dma_start(table_blocks[kb][:], table[kb * P : (kb + 1) * P, :])
-            nc.sync.dma_start(weights[0][:, kb, :], w[0, kb * P : (kb + 1) * P, :])
+            nc.scalar.dma_start(table_blocks[kb][:], table_by_block[kb])
+            nc.sync.dma_start(weights[0][:, kb, :], first_by_block[kb])
         for e in range(1, E):
-            nc.sync.dma_start(weights[e][:], w[e].rearrange("(kb p) m -> p kb m", p=P))
+            nc.sync.dma_start(weights[e][:], w[e].rearrange("(p kb) m -> p kb m", kb=K_BLOCKS))
 
         zeros = held.tile([P, WARM_COLUMNS], BF16, name="zeros")
         nc.vector.memset(zeros[:], 0.0)

import concourse.mybir as mybir

BF16, F32, U16 = mybir.dt.bfloat16, mybir.dt.float32, mybir.dt.uint16
SIGMOID = mybir.ActivationFunctionType.Sigmoid
MULT = mybir.AluOpType.mult

P = 128
S = 256
K = 256
K_BLOCKS = K // P
H = 128
E = 4
Q = 64
N = E * Q
Q_COLS = Q // 16

WARM_MATMULS = 7
WARM_COLUMNS = 256

FLOPS = 2 * K * 2 * H * N


def tile_gather_matmul_kernel(tc, table, w, offs, out):
    nc = tc.nc
    with (
        tc.tile_pool(name="held", bufs=1) as held,
        tc.psum_pool(name="psum", bufs=E) as psum,
    ):
        offsets = held.tile([P, N // 16], U16, name="offsets")
        nc.sync.dma_start(offsets[:], offs)

        table_blocks = [held.tile([P, S], BF16, name=f"table{kb}") for kb in range(K_BLOCKS)]
        weights = [held.tile([P, K_BLOCKS, 2 * H], BF16, name=f"w{e}") for e in range(E)]

        table_by_block = table.rearrange("(p kb) s -> kb p s", kb=K_BLOCKS)
        first_by_block = w[0].rearrange("(p kb) m -> kb p m", kb=K_BLOCKS)
        for kb in range(K_BLOCKS):
            nc.scalar.dma_start(table_blocks[kb][:], table_by_block[kb])
            nc.sync.dma_start(weights[0][:, kb, :], first_by_block[kb])
        for e in range(1, E):
            nc.sync.dma_start(weights[e][:], w[e].rearrange("(p kb) m -> p kb m", kb=K_BLOCKS))

        zeros = held.tile([P, WARM_COLUMNS], BF16, name="zeros")
        nc.vector.memset(zeros[:], 0.0)
        warm = psum.tile([P, WARM_COLUMNS], F32, name="warm", tag="value")
        for i in range(WARM_MATMULS):
            nc.tensor.matmul(warm[:], zeros[:, 0:P], zeros[:], start=True, stop=True)

        for e in range(E):
            picked = offsets[:, e * Q_COLS : (e + 1) * Q_COLS]

            gate = psum.tile([P, Q], F32, name="gate", tag="gate")
            value = psum.tile([P, Q], F32, name="value", tag="value")
            for bank, first_column in ((gate, H), (value, 0)):
                for kb in range(K_BLOCKS):
                    nc.tensor.matmul(
                        bank[:],
                        weights[e][:, kb, first_column : first_column + H],
                        table_blocks[kb][:].indirect(picked),
                        start=(kb == 0),
                        stop=(kb == K_BLOCKS - 1),
                    )

            opened = held.tile([P, Q], F32, name=f"opened{e}")
            nc.scalar.activation(opened[:], gate[:], SIGMOID)
            gated = held.tile([P, Q], F32, name=f"gated{e}")
            nc.vector.tensor_tensor(gated[:], value[:], opened[:], MULT)
            nc.sync.dma_start(out[:, e * Q : (e + 1) * Q], gated[:])
